import numpy as np
import ml_dtypes


def mxq(x, axis, fmt="e4m3"):
    dtype, down = {"e4m3": (ml_dtypes.float8_e4m3fn, 7), "e5m2": (ml_dtypes.float8_e5m2, 14)}[fmt]
    v = np.moveaxis(np.asarray(x, np.float32).astype(ml_dtypes.bfloat16).astype(np.float64), axis, -1)
    blocks = v.reshape(v.shape[:-1] + (-1, 32))
    amax = np.abs(blocks).max(-1, keepdims=True)
    byte = np.maximum(np.where(amax > 0, np.frexp(amax)[1] - 1 + 127, 0) - down, 1)
    scale = np.exp2(byte - 127.0)
    codes = (blocks / scale).astype(np.float32).astype(dtype).astype(np.float64)
    return np.moveaxis((codes * scale).reshape(v.shape), -1, axis)


WIDE = False


def mx_kscale(k):
    if not WIDE:
        return np.ones(k)
    levels = np.array([10, -10, 5, -5, 0])
    if k % 512:
        return np.exp2(np.random.permutation(np.resize(levels, k // 32))).repeat(32)
    a = np.empty((k // 512, 16))
    for p in range(k // 512):
        a[p, :8] = np.random.permutation(np.resize(levels, 8))
        for g in range(8):
            far = levels[np.abs(levels - a[p, g]) >= 10]
            a[p, g + 8] = far[np.random.randint(len(far))]
    return np.exp2(a.ravel()).repeat(32)


def f64(x):
    return np.asarray(x).astype(np.float64)


def striped(idx):
    return np.tile(np.asarray(idx).reshape(-1, 16).T, (8, 1)).astype(np.uint16)


def unstriped(offs):
    return offs[:16].T.reshape(-1).astype(np.int64)


B, N, T, D, DV, NQ = 1, 512, 2048, 256, 512, 1024


def setup_inputs():
    n = np.random.standard_normal
    idx = np.random.permutation(T)[:B * N]
    s = mx_kscale(DV)[:, None]
    z = mx_kscale(NQ)[:, None]
    p = np.exp(n((B, NQ, N)))
    p = p / p.mean(2, keepdims=True)
    return {
        "doT": (n((B, DV, NQ)) * s / np.sqrt(DV)).astype(np.float32),
        "vT": (n((DV, T)) / s).astype(np.float32),
        "p": (p * z / np.sqrt(NQ)).astype(np.float32),
        "delta": (0.3 * n((B, NQ, 1))).astype(np.float32),
        "qm": (n((B, NQ, D)) / z).astype(np.float32),
        "offs": striped(idx),
    }


def reference(doT, vT, p, delta, qm, offs):
    idx = unstriped(offs)
    pick = lambda x: x[:, idx].reshape(x.shape[0], B, N).transpose(1, 0, 2)
    dp = mxq(f64(doT), 1, "e4m3").transpose(0, 2, 1) @ mxq(pick(f64(vT)), 1, "e4m3")
    ds = f64(p) * (dp - f64(delta))
    dk = mxq(f64(qm), 1, "e4m3").transpose(0, 2, 1) @ mxq(ds, 1, "e4m3")
    out = np.zeros((D, T))
    out[:, idx] = dk.transpose(1, 0, 2).reshape(D, B * N)
    return out

@@ -1,0 +1,182 @@
+from contextlib import ExitStack
+
+import concourse.mybir as mybir
+
+N, T, D, DV, NQ = 512, 2048, 256, 512, 1024
+FLOPS = 2 * NQ * N * (DV + D)
+
+F32 = mybir.dt.float32
+BF16 = mybir.dt.bfloat16
+U32 = mybir.dt.uint32
+U16 = mybir.dt.uint16
+U8 = mybir.dt.uint8
+FP8X4 = mybir.dt.float8_e4m3fn_x4
+ACT = mybir.ActivationFunctionType
+ALU = mybir.AluOpType
+
+P = 128
+PACK = 4
+K_PASS = P * PACK
+PASSES = NQ // K_PASS
+HALF = N // 2
+LINE = 4
+
+
+def tile_attend_bwd_kernel(tc, doT, vT, p, delta, qm, offs, out):
+    nc = tc.nc
+
+    with ExitStack() as ctx:
+        keep = ctx.enter_context(tc.tile_pool(name="keep", bufs=1))
+        dp_psum = ctx.enter_context(tc.psum_pool(name="dp_psum", bufs=4))
+        dk_psum = ctx.enter_context(tc.psum_pool(name="dk_psum", bufs=1))
+
+        def quantize(codes, scales, values):
+            nc.vector.quantize_mx(out=codes.bitcast(FP8X4), scales=scales, in_=values)
+
+        def mx_tiles(name, words):
+            codes = keep.tile([P, words], U32, name=name + "_codes", align_bytes=64)
+            scales = keep.tile([P, words], U8, name=name + "_scales", align_bytes=64)
+            return codes, scales
+
+        offsets = keep.tile([P, N // 16], U16, name="offsets")
+        nc.sync.dma_start(offsets[:], offs)
+
+        delta_sb = keep.tile([P, PASSES, 8], F32, name="delta_sb")
+        nc.scalar.dma_start(out=delta_sb[:, :, 0:PACK], in_=delta[0].rearrange("(g p t) o -> p g (t o)", g=PASSES, t=PACK))
+
+        v_rows = vT.rearrange("(p j) n -> p j n", j=PACK)
+        v_plane = []
+        for j in range(PACK):
+            plane = keep.tile([P, T], F32, name="v_plane%d" % j)
+            nc.sync.dma_start(out=plane[:], in_=v_rows[:, j, :])
+            v_plane.append(plane)
+
+        do_rows = doT[0].rearrange("(p j) q -> p j q", j=PACK)
+        do_raw = []
+        for g in range(PASSES):
+            raw = keep.tile([P, PACK, K_PASS], F32, name="do_raw%d" % g)
+            nc.sync.dma_start(out=raw[:], in_=do_rows[:, :, g * K_PASS : (g + 1) * K_PASS])
+            do_raw.append(raw)
+
+        p_rows = p[0].rearrange("(g p t) n -> g p t n", g=PASSES, t=PACK)
+        q_rows = qm[0].rearrange("(g p t) d -> g p t d", g=PASSES, t=PACK)
+        p0 = keep.tile([P, PACK, N], F32, name="p0")
+        nc.sync.dma_start(out=p0[:], in_=p_rows[0])
+        p1a = keep.tile([P, PACK, HALF], F32, name="p1a")
+        nc.sync.dma_start(out=p1a[:], in_=p_rows[1][:, :, 0:HALF])
+        q_raw = []
+        for g in range(PASSES):
+            raw = keep.tile([P, PACK, D], F32, name="q_raw%d" % g)
+            nc.sync.dma_start(out=raw[:], in_=q_rows[g])
+            q_raw.append(raw)
+        p1b = keep.tile([P, PACK, HALF], F32, name="p1b")
+        nc.sync.dma_start(out=p1b[:], in_=p_rows[1][:, :, HALF:N])
+
+        window = []
+        for h in range(D // P):
+            win = keep.tile([P, T], F32, name="window%d" % h)
+            nc.vector.memset(win[:], 0.0)
+            window.append(win)
+
+        neg_delta = keep.tile([P, PASSES, PACK], F32, name="neg_delta")
+        nc.scalar.activation(out=neg_delta[:], in_=delta_sb[:, :, 0:PACK], func=ACT.Copy, scale=-1.0)
+
+        v_bf = keep.tile([P, N, PACK], BF16, name="v_bf", align_bytes=64)
+        for j in range(PACK):
+            nc.vector.tensor_copy(v_bf[:, :, j], v_plane[j][:].indirect(offsets[:]))
+        v_codes, v_scales = mx_tiles("v", N)
+        quantize(v_codes[:], v_scales[:], v_bf[:].rearrange("p n j -> p (n j)"))
+
+        dpd = []
+        for g in range(PASSES):
+            do_bf = keep.tile([P, PACK, P, PACK], BF16, name="do_bf%d" % g, align_bytes=64)
+            nc.vector.tensor_copy(
+                out=do_bf[:].rearrange("p t m j -> p m j t"),
+                in_=do_raw[g][:].rearrange("p j (m t) -> p m j t", t=PACK),
+            )
+            do_codes, do_scales = mx_tiles("do%d" % g, K_PASS)
+            quantize(do_codes[:], do_scales[:], do_bf[:].rearrange("p t m j -> p (t m j)"))
+            shifted = keep.tile([P, PACK, N], F32, name="dpd%d" % g)
+            for t in range(PACK):
+                cols = slice(t * P, (t + 1) * P)
+                dp = dp_psum.tile([P, N], F32, name="dp")
+                nc.tensor.matmul_mx(
+                    out=dp[:],
+                    lhsT=do_codes[:, cols].bitcast(FP8X4),
+                    lhsT_scale=do_scales[:, cols],
+                    rhs=v_codes[:].bitcast(FP8X4),
+                    rhs_scale=v_scales[:],
+                    start=True,
+                    stop=True,
+                )
+                nc.scalar.activation(
+                    out=shifted[:, t, :], in_=dp[:], func=ACT.Identity, bias=neg_delta[:, g, t : t + 1], scale=1.0
+                )
+            dpd.append(shifted)
+
+        q_bf = []
+        for h in range(D // P):
+            grouped = keep.tile([P, PASSES, P, PACK], BF16, name="q_bf%d" % h, align_bytes=64)
+            for g in range(PASSES):
+                nc.scalar.copy(
+                    out=grouped[:, g, :, :].rearrange("p (c i) t -> p c t i", i=LINE),
+                    in_=q_raw[g][:, :, h * P : (h + 1) * P].rearrange("p t (c i) -> p c t i", i=LINE),
+                )
+            q_bf.append(grouped)
+        q_mx = [mx_tiles("q%d" % h, PASSES * P) for h in range(D // P)]
+
+        def quantize_q(h):
+            quantize(q_mx[h][0][:], q_mx[h][1][:], q_bf[h][:].rearrange("p g d t -> p (g d t)"))
+
+        ds_bf = [keep.tile([P, N, PACK], BF16, name="ds_bf%d" % g, align_bytes=64) for g in range(PASSES)]
+        ds_mx = [mx_tiles("ds%d" % g, N) for g in range(PASSES)]
+
+        def form_ds(g, slots, weights):
+            nc.vector.tensor_tensor(
+                out=ds_bf[g][:, slots, :].rearrange("p (c i) t -> p c t i", i=LINE),
+                in0=dpd[g][:, :, slots].rearrange("p t (c i) -> p c t i", i=LINE),
+                in1=weights.rearrange("p t (c i) -> p c t i", i=LINE),
+                op=ALU.mult,
+            )
+
+        def quantize_ds(g, slots):
+            quantize(ds_mx[g][0][:, slots], ds_mx[g][1][:, slots], ds_bf[g][:, slots, :].rearrange("p n t -> p (n t)"))
+
+        def product(h, slots, name):
+            width = slots.stop - slots.start
+            acc = dk_psum.tile([P, width], F32, name=name + "_acc")
+            for g in range(PASSES):
+                cols = slice(g * P, (g + 1) * P)
+                nc.tensor.matmul_mx(
+                    out=acc[:],
+                    lhsT=q_mx[h][0][:, cols].bitcast(FP8X4),
+                    lhsT_scale=q_mx[h][1][:, cols],
+                    rhs=ds_mx[g][0][:, slots].bitcast(FP8X4),
+                    rhs_scale=ds_mx[g][1][:, slots],
+                    start=(g == 0),
+                    stop=(g == PASSES - 1),
+                )
+            dk = keep.tile([P, width], F32, name=name)
+            nc.scalar.copy(out=dk[:], in_=acc[:])
+            return dk
+
+        def scatter(h, slots, dk):
+            nc.vector.tensor_copy(window[h][:].indirect(offsets[:, slots.start // 16 : slots.stop // 16]), dk[:])
+
+        whole, first, second = slice(0, N), slice(0, HALF), slice(HALF, N)
+        form_ds(0, whole, p0[:])
+        form_ds(1, first, p1a[:])
+        quantize_ds(0, whole)
+        quantize_q(0)
+        quantize_ds(1, first)
+        dk0a = product(0, first, "dk0a")
+        form_ds(1, second, p1b[:])
+        quantize_q(1)
+        quantize_ds(1, second)
+        dk0b = product(0, second, "dk0b")
+        dk1 = product(1, whole, "dk1")
+        scatter(0, first, dk0a)
+        scatter(0, second, dk0b)
+        nc.sync.dma_start(out=out[0:P, :], in_=window[0][:])
+        scatter(1, whole, dk1)
+        nc.sync.dma_start(out=out[P : 2 * P, :], in_=window[1][:])

@@ -20,6 +20,7 @@ K_PASS = P * PACK
 PASSES = NQ // K_PASS
 HALF = N // 2
 LINE = 4
+SPLIT = 80
 
 
 def tile_attend_bwd_kernel(tc, doT, vT, p, delta, qm, offs, out):
@@ -27,15 +28,15 @@ def tile_attend_bwd_kernel(tc, doT, vT, p, delta, qm, offs, out):
 
     with ExitStack() as ctx:
         keep = ctx.enter_context(tc.tile_pool(name="keep", bufs=1))
-        dp_psum = ctx.enter_context(tc.psum_pool(name="dp_psum", bufs=4))
+        dp_psum = ctx.enter_context(tc.psum_pool(name="dp_psum", bufs=5))
         dk_psum = ctx.enter_context(tc.psum_pool(name="dk_psum", bufs=1))
 
         def quantize(codes, scales, values):
             nc.vector.quantize_mx(out=codes.bitcast(FP8X4), scales=scales, in_=values)
 
         def mx_tiles(name, words):
-            codes = keep.tile([P, words], U32, name=name + "_codes", align_bytes=64)
-            scales = keep.tile([P, words], U8, name=name + "_scales", align_bytes=64)
+            codes = keep.tile([P, words], U32, name=name + "_codes", tag=name + "_codes", align_bytes=64)
+            scales = keep.tile([P, words], U8, name=name + "_scales", tag=name + "_scales", align_bytes=64)
             return codes, scales
 
         offsets = keep.tile([P, N // 16], U16, name="offsets")
@@ -53,9 +54,9 @@ def tile_attend_bwd_kernel(tc, doT, vT, p, delta, qm, offs, out):
 
         do_rows = doT[0].rearrange("(p j) q -> p j q", j=PACK)
         do_raw = []
-        for g in range(PASSES):
-            raw = keep.tile([P, PACK, K_PASS], F32, name="do_raw%d" % g)
-            nc.sync.dma_start(out=raw[:], in_=do_rows[:, :, g * K_PASS : (g + 1) * K_PASS])
+        for name, q0, q1 in (("do0", 0, 512), ("do1", 512, 1024)):
+            raw = keep.tile([P, PACK, q1 - q0], F32, name=name)
+            nc.sync.dma_start(out=raw[:], in_=do_rows[:, :, q0:q1])
             do_raw.append(raw)
 
         p_rows = p[0].rearrange("(g p t) n -> g p t n", g=PASSES, t=PACK)
@@ -69,7 +70,7 @@ def tile_attend_bwd_kernel(tc, doT, vT, p, delta, qm, offs, out):
             raw = keep.tile([P, PACK, D], F32, name="q_raw%d" % g)
             nc.sync.dma_start(out=raw[:], in_=q_rows[g])
             q_raw.append(raw)
-        p1b = keep.tile([P, PACK, HALF], F32, name="p1b")
+        p1b = keep.tile([P, PACK, HALF], F32, name="p1b", tag="dk0a")
         nc.sync.dma_start(out=p1b[:], in_=p_rows[1][:, :, HALF:N])
 
         window = []
@@ -87,45 +88,70 @@ def tile_attend_bwd_kernel(tc, doT, vT, p, delta, qm, offs, out):
         v_codes, v_scales = mx_tiles("v", N)
         quantize(v_codes[:], v_scales[:], v_bf[:].rearrange("p n j -> p (n j)"))
 
-        dpd = []
-        for g in range(PASSES):
-            do_bf = keep.tile([P, PACK, P, PACK], BF16, name="do_bf%d" % g, align_bytes=64)
-            nc.vector.tensor_copy(
-                out=do_bf[:].rearrange("p t m j -> p m j t"),
-                in_=do_raw[g][:].rearrange("p j (m t) -> p m j t", t=PACK),
-            )
-            do_codes, do_scales = mx_tiles("do%d" % g, K_PASS)
-            quantize(do_codes[:], do_scales[:], do_bf[:].rearrange("p t m j -> p (t m j)"))
-            shifted = keep.tile([P, PACK, N], F32, name="dpd%d" % g)
-            for t in range(PACK):
-                cols = slice(t * P, (t + 1) * P)
-                dp = dp_psum.tile([P, N], F32, name="dp")
-                nc.tensor.matmul_mx(
-                    out=dp[:],
-                    lhsT=do_codes[:, cols].bitcast(FP8X4),
-                    lhsT_scale=do_scales[:, cols],
-                    rhs=v_codes[:].bitcast(FP8X4),
-                    rhs_scale=v_scales[:],
-                    start=True,
-                    stop=True,
-                )
-                nc.scalar.activation(
-                    out=shifted[:, t, :], in_=dp[:], func=ACT.Identity, bias=neg_delta[:, g, t : t + 1], scale=1.0
-                )
-            dpd.append(shifted)
+        whole, first, second = slice(0, N), slice(0, HALF), slice(HALF, N)
 
-        q_bf = []
-        for h in range(D // P):
-            grouped = keep.tile([P, PASSES, P, PACK], BF16, name="q_bf%d" % h, align_bytes=64)
+        def group_do(copy, do_bf, cols, raw, raw_cols):
+            copy(
+                out=do_bf[:].rearrange("p t m j -> p m j t")[:, cols],
+                in_=raw[:].rearrange("p j (m t) -> p m j t", t=PACK)[:, raw_cols],
+            )
+
+        do_bf = [keep.tile([P, PACK, P, PACK], BF16, name="do_bf%d" % g, align_bytes=64) for g in range(PASSES)]
+        do_mx = [mx_tiles("do%d" % g, K_PASS) for g in range(PASSES)]
+        dpd = [
+            keep.tile([P, PACK, N], F32, name="dpd%d" % g, tag=("dpd0", "q1_codes")[g], align_bytes=64)
+            for g in range(PASSES)
+        ]
+
+        def quantize_do(g):
+            flat = do_bf[g][:].rearrange("p t m j -> p (t m j)")
+            for u in range(2):
+                words = slice(u * 256, (u + 1) * 256)
+                quantize(do_mx[g][0][:, words], do_mx[g][1][:, words], flat[:, u * 1024 : (u + 1) * 1024])
+
+        def dp_matmul(g, t, slots):
+            cols = slice(t * P, (t + 1) * P)
+            dp = dp_psum.tile([P, slots.stop - slots.start], F32, name="dp")
+            nc.tensor.matmul_mx(
+                out=dp[:],
+                lhsT=do_mx[g][0][:, cols].bitcast(FP8X4),
+                lhsT_scale=do_mx[g][1][:, cols],
+                rhs=v_codes[:, slots].bitcast(FP8X4),
+                rhs_scale=v_scales[:, slots],
+                start=True,
+                stop=True,
+            )
+            return dp
+
+        def shift(g, t, slots, dp):
+            nc.scalar.activation(
+                out=dpd[g][:, t, slots], in_=dp[:], func=ACT.Identity, bias=neg_delta[:, g, t : t + 1], scale=1.0
+            )
+
+        group_do(nc.vector.tensor_copy, do_bf[0], slice(0, SPLIT), do_raw[0], slice(0, SPLIT))
+        group_do(nc.scalar.copy, do_bf[0], slice(SPLIT, P), do_raw[0], slice(SPLIT, P))
+        quantize_do(0)
+        group_do(nc.vector.tensor_copy, do_bf[1], slice(0, P), do_raw[1], slice(0, P))
+        quantize_do(1)
+
+        for g, slots in ((0, whole), (1, first), (1, second)):
+            for t in range(PACK):
+                shift(g, t, slots, dp_matmul(g, t, slots))
+
+        def group_q(h):
+            grouped = keep.tile([P, PASSES, P, PACK], BF16, name="q_bf%d" % h, tag=("do1_codes", "do1_scales")[h], align_bytes=64)
             for g in range(PASSES):
                 nc.scalar.copy(
                     out=grouped[:, g, :, :].rearrange("p (c i) t -> p c t i", i=LINE),
                     in_=q_raw[g][:, :, h * P : (h + 1) * P].rearrange("p t (c i) -> p c t i", i=LINE),
                 )
-            q_bf.append(grouped)
-        q_mx = [mx_tiles("q%d" % h, PASSES * P) for h in range(D // P)]
+            return grouped
+
+        q_bf = [group_q(h) for h in range(D // P)]
+        q_mx = {}
 
         def quantize_q(h):
+            q_mx[h] = mx_tiles("q%d" % h, PASSES * P)
             quantize(q_mx[h][0][:], q_mx[h][1][:], q_bf[h][:].rearrange("p g d t -> p (g d t)"))
 
         ds_bf = [keep.tile([P, N, PACK], BF16, name="ds_bf%d" % g, align_bytes=64) for g in range(PASSES)]
@@ -135,7 +161,7 @@ def tile_attend_bwd_kernel(tc, doT, vT, p, delta, qm, offs, out):
             nc.vector.tensor_tensor(
                 out=ds_bf[g][:, slots, :].rearrange("p (c i) t -> p c t i", i=LINE),
                 in0=dpd[g][:, :, slots].rearrange("p t (c i) -> p c t i", i=LINE),
-                in1=weights.rearrange("p t (c i) -> p c t i", i=LINE),
+                in1=weights[:].rearrange("p t (c i) -> p c t i", i=LINE),
                 op=ALU.mult,
             )
 
@@ -156,23 +182,22 @@ def tile_attend_bwd_kernel(tc, doT, vT, p, delta, qm, offs, out):
                     start=(g == 0),
                     stop=(g == PASSES - 1),
                 )
-            dk = keep.tile([P, width], F32, name=name)
+            dk = keep.tile([P, width], F32, name=name, tag=name)
             nc.scalar.copy(out=dk[:], in_=acc[:])
             return dk
 
         def scatter(h, slots, dk):
             nc.vector.tensor_copy(window[h][:].indirect(offsets[:, slots.start // 16 : slots.stop // 16]), dk[:])
 
-        whole, first, second = slice(0, N), slice(0, HALF), slice(HALF, N)
-        form_ds(0, whole, p0[:])
-        form_ds(1, first, p1a[:])
+        form_ds(0, whole, p0)
+        form_ds(1, first, p1a)
         quantize_ds(0, whole)
-        quantize_q(0)
         quantize_ds(1, first)
+        quantize_q(0)
+        form_ds(1, second, p1b)
         dk0a = product(0, first, "dk0a")
-        form_ds(1, second, p1b[:])
-        quantize_q(1)
         quantize_ds(1, second)
+        quantize_q(1)
         dk0b = product(0, second, "dk0b")
         dk1 = product(1, whole, "dk1")
         scatter(0, first, dk0a)

@@ -40,7 +40,6 @@ def tile_attend_bwd_kernel(tc, doT, vT, p, delta, qm, offs, out):
             return codes, scales
 
         offsets = keep.tile([P, N // 16], U16, name="offsets")
-        nc.sync.dma_start(offsets[:], offs)
 
         delta_sb = keep.tile([P, PASSES, 8], F32, name="delta_sb")
         nc.scalar.dma_start(out=delta_sb[:, :, 0:PACK], in_=delta[0].rearrange("(g p t) o -> p g (t o)", g=PASSES, t=PACK))
@@ -50,28 +49,36 @@ def tile_attend_bwd_kernel(tc, doT, vT, p, delta, qm, offs, out):
         for j in range(PACK):
             plane = keep.tile([P, T], F32, name="v_plane%d" % j)
             nc.sync.dma_start(out=plane[:], in_=v_rows[:, j, :])
+            if j == 0:
+                nc.sync.dma_start(offsets[:], offs)
             v_plane.append(plane)
 
         do_rows = doT[0].rearrange("(p j) q -> p j q", j=PACK)
         do_raw = []
-        for name, q0, q1 in (("do0", 0, 512), ("do1", 512, 1024)):
+        for name, q0, q1 in (("do0", 0, 512), ("do1a", 512, 768), ("do1b", 768, 1024)):
             raw = keep.tile([P, PACK, q1 - q0], F32, name=name)
             nc.sync.dma_start(out=raw[:], in_=do_rows[:, :, q0:q1])
             do_raw.append(raw)
 
         p_rows = p[0].rearrange("(g p t) n -> g p t n", g=PASSES, t=PACK)
         q_rows = qm[0].rearrange("(g p t) d -> g p t d", g=PASSES, t=PACK)
-        p0 = keep.tile([P, PACK, N], F32, name="p0")
-        nc.sync.dma_start(out=p0[:], in_=p_rows[0])
+        p0a = keep.tile([P, PACK, HALF], F32, name="p0a")
+        nc.sync.dma_start(out=p0a[:], in_=p_rows[0][:, :, 0:HALF])
+        p0b = keep.tile([P, PACK, HALF], F32, name="p0b")
+        nc.sync.dma_start(out=p0b[:], in_=p_rows[0][:, :, HALF:N])
         p1a = keep.tile([P, PACK, HALF], F32, name="p1a")
         nc.sync.dma_start(out=p1a[:], in_=p_rows[1][:, :, 0:HALF])
-        q_raw = []
-        for g in range(PASSES):
-            raw = keep.tile([P, PACK, D], F32, name="q_raw%d" % g)
-            nc.sync.dma_start(out=raw[:], in_=q_rows[g])
-            q_raw.append(raw)
-        p1b = keep.tile([P, PACK, HALF], F32, name="p1b", tag="dk0a")
+        q_raw = {}
+
+        def load_q(h):
+            for g in range(PASSES):
+                q_raw[h, g] = keep.tile([P, PACK, P], F32, name="q_raw%d%d" % (h, g))
+                nc.sync.dma_start(out=q_raw[h, g][:], in_=q_rows[g][:, :, h * P : (h + 1) * P])
+
+        load_q(0)
+        p1b = keep.tile([P, PACK, HALF], F32, name="p1b", tag="q1_codes", align_bytes=64)
         nc.sync.dma_start(out=p1b[:], in_=p_rows[1][:, :, HALF:N])
+        load_q(1)
 
         window = []
         for h in range(D // P):
@@ -98,10 +105,7 @@ def tile_attend_bwd_kernel(tc, doT, vT, p, delta, qm, offs, out):
 
         do_bf = [keep.tile([P, PACK, P, PACK], BF16, name="do_bf%d" % g, align_bytes=64) for g in range(PASSES)]
         do_mx = [mx_tiles("do%d" % g, K_PASS) for g in range(PASSES)]
-        dpd = [
-            keep.tile([P, PACK, N], F32, name="dpd%d" % g, tag=("dpd0", "q1_codes")[g], align_bytes=64)
-            for g in range(PASSES)
-        ]
+        dpd = [keep.tile([P, PACK, N], F32, name="dpd%d" % g) for g in range(PASSES)]
 
         def quantize_do(g):
             flat = do_bf[g][:].rearrange("p t m j -> p (t m j)")
@@ -131,46 +135,47 @@ def tile_attend_bwd_kernel(tc, doT, vT, p, delta, qm, offs, out):
         group_do(nc.vector.tensor_copy, do_bf[0], slice(0, SPLIT), do_raw[0], slice(0, SPLIT))
         group_do(nc.scalar.copy, do_bf[0], slice(SPLIT, P), do_raw[0], slice(SPLIT, P))
         quantize_do(0)
-        group_do(nc.vector.tensor_copy, do_bf[1], slice(0, P), do_raw[1], slice(0, P))
+        group_do(nc.scalar.copy, do_bf[1], slice(0, 64), do_raw[1], slice(0, 64))
+        group_do(nc.vector.tensor_copy, do_bf[1], slice(64, P), do_raw[2], slice(0, 64))
         quantize_do(1)
 
-        for g, slots in ((0, whole), (1, first), (1, second)):
+        for g, slots in ((0, first), (0, second), (1, first), (1, second)):
             for t in range(PACK):
                 shift(g, t, slots, dp_matmul(g, t, slots))
 
+        q_bf = {}
+
         def group_q(h):
-            grouped = keep.tile([P, PASSES, P, PACK], BF16, name="q_bf%d" % h, tag=("do1_codes", "do1_scales")[h], align_bytes=64)
+            q_bf[h] = keep.tile(
+                [P, PASSES, P, PACK], BF16, name="q_bf%d" % h, tag=("do1_codes", "do1_scales")[h], align_bytes=64
+            )
             for g in range(PASSES):
                 nc.scalar.copy(
-                    out=grouped[:, g, :, :].rearrange("p (c i) t -> p c t i", i=LINE),
-                    in_=q_raw[g][:, :, h * P : (h + 1) * P].rearrange("p t (c i) -> p c t i", i=LINE),
+                    out=q_bf[h][:, g, :, :].rearrange("p (c i) t -> p c t i", i=LINE),
+                    in_=q_raw[h, g][:].rearrange("p t (c i) -> p c t i", i=LINE),
                 )
-            return grouped
 
-        q_bf = [group_q(h) for h in range(D // P)]
         q_mx = {}
 
         def quantize_q(h):
             q_mx[h] = mx_tiles("q%d" % h, PASSES * P)
             quantize(q_mx[h][0][:], q_mx[h][1][:], q_bf[h][:].rearrange("p g d t -> p (g d t)"))
 
-        ds_bf = [keep.tile([P, N, PACK], BF16, name="ds_bf%d" % g, align_bytes=64) for g in range(PASSES)]
         ds_mx = [mx_tiles("ds%d" % g, N) for g in range(PASSES)]
 
-        def form_ds(g, slots, weights):
+        def form_ds(g, slots, weights, ds):
             nc.vector.tensor_tensor(
-                out=ds_bf[g][:, slots, :].rearrange("p (c i) t -> p c t i", i=LINE),
+                out=ds.rearrange("p (c i) t -> p c t i", i=LINE),
                 in0=dpd[g][:, :, slots].rearrange("p t (c i) -> p c t i", i=LINE),
-                in1=weights[:].rearrange("p t (c i) -> p c t i", i=LINE),
+                in1=weights.rearrange("p t (c i) -> p c t i", i=LINE),
                 op=ALU.mult,
             )
 
-        def quantize_ds(g, slots):
-            quantize(ds_mx[g][0][:, slots], ds_mx[g][1][:, slots], ds_bf[g][:, slots, :].rearrange("p n t -> p (n t)"))
+        def quantize_ds(g, slots, ds):
+            quantize(ds_mx[g][0][:, slots], ds_mx[g][1][:, slots], ds.rearrange("p n t -> p (n t)"))
 
-        def product(h, slots, name):
-            width = slots.stop - slots.start
-            acc = dk_psum.tile([P, width], F32, name=name + "_acc")
+        def product(h, slots, bank, dk):
+            acc = dk_psum.tile([P, HALF], F32, name="dk_acc", tag=bank)
             for g in range(PASSES):
                 cols = slice(g * P, (g + 1) * P)
                 nc.tensor.matmul_mx(
@@ -182,25 +187,32 @@ def tile_attend_bwd_kernel(tc, doT, vT, p, delta, qm, offs, out):
                     start=(g == 0),
                     stop=(g == PASSES - 1),
                 )
-            dk = keep.tile([P, width], F32, name=name, tag=name)
-            nc.scalar.copy(out=dk[:], in_=acc[:])
-            return dk
+            nc.scalar.copy(out=dk, in_=acc[:])
 
         def scatter(h, slots, dk):
             nc.vector.tensor_copy(window[h][:].indirect(offsets[:, slots.start // 16 : slots.stop // 16]), dk[:])
 
-        form_ds(0, whole, p0)
-        form_ds(1, first, p1a)
-        quantize_ds(0, whole)
-        quantize_ds(1, first)
+        ds = [keep.tile([P, N, PACK], BF16, name="ds%d" % g, align_bytes=64) for g in range(PASSES)]
+        group_q(0)
+        form_ds(0, first, p0a[:], ds[0][:, first, :])
+        form_ds(0, second, p0b[:], ds[0][:, second, :])
+        quantize_ds(0, first, ds[0][:, first, :])
+        form_ds(1, first, p1a[:], ds[1][:, first, :])
         quantize_q(0)
-        form_ds(1, second, p1b)
-        dk0a = product(0, first, "dk0a")
-        quantize_ds(1, second)
-        quantize_q(1)
-        dk0b = product(0, second, "dk0b")
-        dk1 = product(1, whole, "dk1")
+        quantize_ds(1, first, ds[1][:, first, :])
+        form_ds(1, second, p1b[:], ds[1][:, second, :])
+        dk0a = keep.tile([P, HALF], F32, name="dk0a", tag="q1_codes", align_bytes=64)
+        product(0, first, "bank0", dk0a[:])
+        quantize_ds(0, second, ds[0][:, second, :])
+        quantize_ds(1, second, ds[1][:, second, :])
+        dk0b = keep.tile([P, HALF], F32, name="dk0b")
+        product(0, second, "bank1", dk0b[:])
+        group_q(1)
         scatter(0, first, dk0a)
+        quantize_q(1)
+        dk1 = keep.tile([P, N], F32, name="dk1")
+        product(1, first, "bank0", dk1[:, first])
+        product(1, second, "bank2", dk1[:, second])
         scatter(0, second, dk0b)
         nc.sync.dma_start(out=out[0:P, :], in_=window[0][:])
         scatter(1, whole, dk1)

@@ -105,7 +105,7 @@ def tile_attend_bwd_kernel(tc, doT, vT, p, delta, qm, offs, out):
 
         do_bf = [keep.tile([P, PACK, P, PACK], BF16, name="do_bf%d" % g, align_bytes=64) for g in range(PASSES)]
         do_mx = [mx_tiles("do%d" % g, K_PASS) for g in range(PASSES)]
-        dpd = [keep.tile([P, PACK, N], F32, name="dpd%d" % g) for g in range(PASSES)]
+        dpd = [keep.tile([P, PACK, N], F32, name="dpd%d" % g, tag=("dpd0", "dk0a")[g]) for g in range(PASSES)]
 
         def quantize_do(g):
             flat = do_bf[g][:].rearrange("p t m j -> p (t m j)")
@@ -201,15 +201,15 @@ def tile_attend_bwd_kernel(tc, doT, vT, p, delta, qm, offs, out):
         quantize_q(0)
         quantize_ds(1, first, ds[1][:, first, :])
         form_ds(1, second, p1b[:], ds[1][:, second, :])
-        dk0a = keep.tile([P, HALF], F32, name="dk0a", tag="q1_codes", align_bytes=64)
+        dk0a = keep.tile([P, HALF], F32, name="dk0a", tag="dk0a")
         product(0, first, "bank0", dk0a[:])
         quantize_ds(0, second, ds[0][:, second, :])
         quantize_ds(1, second, ds[1][:, second, :])
         dk0b = keep.tile([P, HALF], F32, name="dk0b")
         product(0, second, "bank1", dk0b[:])
         group_q(1)
-        scatter(0, first, dk0a)
         quantize_q(1)
+        scatter(0, first, dk0a)
         dk1 = keep.tile([P, N], F32, name="dk1")
         product(1, first, "bank0", dk1[:, first])
         product(1, second, "bank2", dk1[:, second])

from contextlib import ExitStack

import concourse.mybir as mybir

N, T, D, DV, NQ = 512, 2048, 256, 512, 1024
FLOPS = 2 * NQ * N * (DV + D)

F32 = mybir.dt.float32
BF16 = mybir.dt.bfloat16
U32 = mybir.dt.uint32
U16 = mybir.dt.uint16
U8 = mybir.dt.uint8
FP8X4 = mybir.dt.float8_e4m3fn_x4
ACT = mybir.ActivationFunctionType
ALU = mybir.AluOpType

P = 128
PACK = 4
K_PASS = P * PACK
PASSES = NQ // K_PASS
HALF = N // 2
LINE = 4
SPLIT = 80


def tile_attend_bwd_kernel(tc, doT, vT, p, delta, qm, offs, out):
    nc = tc.nc

    with ExitStack() as ctx:
        keep = ctx.enter_context(tc.tile_pool(name="keep", bufs=1))
        dp_psum = ctx.enter_context(tc.psum_pool(name="dp_psum", bufs=5))
        dk_psum = ctx.enter_context(tc.psum_pool(name="dk_psum", bufs=1))

        def quantize(codes, scales, values):
            nc.vector.quantize_mx(out=codes.bitcast(FP8X4), scales=scales, in_=values)

        def mx_tiles(name, words):
            codes = keep.tile([P, words], U32, name=name + "_codes", tag=name + "_codes", align_bytes=64)
            scales = keep.tile([P, words], U8, name=name + "_scales", tag=name + "_scales", align_bytes=64)
            return codes, scales

        offsets = keep.tile([P, N // 16], U16, name="offsets")

        delta_sb = keep.tile([P, PASSES, 8], F32, name="delta_sb")
        nc.scalar.dma_start(out=delta_sb[:, :, 0:PACK], in_=delta[0].rearrange("(g p t) o -> p g (t o)", g=PASSES, t=PACK))

        v_rows = vT.rearrange("(p j) n -> p j n", j=PACK)
        v_plane = []
        for j in range(PACK):
            plane = keep.tile([P, T], F32, name="v_plane%d" % j)
            nc.sync.dma_start(out=plane[:], in_=v_rows[:, j, :])
            if j == 0:
                nc.sync.dma_start(offsets[:], offs)
            v_plane.append(plane)

        do_rows = doT[0].rearrange("(p j) q -> p j q", j=PACK)
        do_raw = []
        for name, q0, q1 in (("do0", 0, 512), ("do1a", 512, 768), ("do1b", 768, 1024)):
            raw = keep.tile([P, PACK, q1 - q0], F32, name=name)
            nc.sync.dma_start(out=raw[:], in_=do_rows[:, :, q0:q1])
            do_raw.append(raw)

        p_rows = p[0].rearrange("(g p t) n -> g p t n", g=PASSES, t=PACK)
        q_rows = qm[0].rearrange("(g p t) d -> g p t d", g=PASSES, t=PACK)
        p0a = keep.tile([P, PACK, HALF], F32, name="p0a")
        nc.sync.dma_start(out=p0a[:], in_=p_rows[0][:, :, 0:HALF])
        p0b = keep.tile([P, PACK, HALF], F32, name="p0b")
        nc.sync.dma_start(out=p0b[:], in_=p_rows[0][:, :, HALF:N])
        p1a = keep.tile([P, PACK, HALF], F32, name="p1a")
        nc.sync.dma_start(out=p1a[:], in_=p_rows[1][:, :, 0:HALF])
        q_raw = {}

        def load_q(h):
            for g in range(PASSES):
                q_raw[h, g] = keep.tile([P, PACK, P], F32, name="q_raw%d%d" % (h, g))
                nc.sync.dma_start(out=q_raw[h, g][:], in_=q_rows[g][:, :, h * P : (h + 1) * P])

        load_q(0)
        p1b = keep.tile([P, PACK, HALF], F32, name="p1b", tag="q1_codes", align_bytes=64)
        nc.sync.dma_start(out=p1b[:], in_=p_rows[1][:, :, HALF:N])
        load_q(1)

        window = []
        for h in range(D // P):
            win = keep.tile([P, T], F32, name="window%d" % h)
            nc.vector.memset(win[:], 0.0)
            window.append(win)

        neg_delta = keep.tile([P, PASSES, PACK], F32, name="neg_delta")
        nc.scalar.activation(out=neg_delta[:], in_=delta_sb[:, :, 0:PACK], func=ACT.Copy, scale=-1.0)

        v_bf = keep.tile([P, N, PACK], BF16, name="v_bf", align_bytes=64)
        for j in range(PACK):
            nc.vector.tensor_copy(v_bf[:, :, j], v_plane[j][:].indirect(offsets[:]))
        v_codes, v_scales = mx_tiles("v", N)
        quantize(v_codes[:], v_scales[:], v_bf[:].rearrange("p n j -> p (n j)"))

        whole, first, second = slice(0, N), slice(0, HALF), slice(HALF, N)

        def group_do(copy, do_bf, cols, raw, raw_cols):
            copy(
                out=do_bf[:].rearrange("p t m j -> p m j t")[:, cols],
                in_=raw[:].rearrange("p j (m t) -> p m j t", t=PACK)[:, raw_cols],
            )

        do_bf = [keep.tile([P, PACK, P, PACK], BF16, name="do_bf%d" % g, align_bytes=64) for g in range(PASSES)]
        do_mx = [mx_tiles("do%d" % g, K_PASS) for g in range(PASSES)]
        dpd = [keep.tile([P, PACK, N], F32, name="dpd%d" % g, tag=("dpd0", "dk0a")[g]) for g in range(PASSES)]

        def quantize_do(g):
            flat = do_bf[g][:].rearrange("p t m j -> p (t m j)")
            for u in range(2):
                words = slice(u * 256, (u + 1) * 256)
                quantize(do_mx[g][0][:, words], do_mx[g][1][:, words], flat[:, u * 1024 : (u + 1) * 1024])

        def dp_matmul(g, t, slots):
            cols = slice(t * P, (t + 1) * P)
            dp = dp_psum.tile([P, slots.stop - slots.start], F32, name="dp")
            nc.tensor.matmul_mx(
                out=dp[:],
                lhsT=do_mx[g][0][:, cols].bitcast(FP8X4),
                lhsT_scale=do_mx[g][1][:, cols],
                rhs=v_codes[:, slots].bitcast(FP8X4),
                rhs_scale=v_scales[:, slots],
                start=True,
                stop=True,
            )
            return dp

        def shift(g, t, slots, dp):
            nc.scalar.activation(
                out=dpd[g][:, t, slots], in_=dp[:], func=ACT.Identity, bias=neg_delta[:, g, t : t + 1], scale=1.0
            )

        group_do(nc.vector.tensor_copy, do_bf[0], slice(0, SPLIT), do_raw[0], slice(0, SPLIT))
        group_do(nc.scalar.copy, do_bf[0], slice(SPLIT, P), do_raw[0], slice(SPLIT, P))
        quantize_do(0)
        group_do(nc.scalar.copy, do_bf[1], slice(0, 64), do_raw[1], slice(0, 64))
        group_do(nc.vector.tensor_copy, do_bf[1], slice(64, P), do_raw[2], slice(0, 64))
        quantize_do(1)

        for g, slots in ((0, first), (0, second), (1, first), (1, second)):
            for t in range(PACK):
                shift(g, t, slots, dp_matmul(g, t, slots))

        q_bf = {}

        def group_q(h):
            q_bf[h] = keep.tile(
                [P, PASSES, P, PACK], BF16, name="q_bf%d" % h, tag=("do1_codes", "do1_scales")[h], align_bytes=64
            )
            for g in range(PASSES):
                nc.scalar.copy(
                    out=q_bf[h][:, g, :, :].rearrange("p (c i) t -> p c t i", i=LINE),
                    in_=q_raw[h, g][:].rearrange("p t (c i) -> p c t i", i=LINE),
                )

        q_mx = {}

        def quantize_q(h):
            q_mx[h] = mx_tiles("q%d" % h, PASSES * P)
            quantize(q_mx[h][0][:], q_mx[h][1][:], q_bf[h][:].rearrange("p g d t -> p (g d t)"))

        ds_mx = [mx_tiles("ds%d" % g, N) for g in range(PASSES)]

        def form_ds(g, slots, weights, ds):
            nc.vector.tensor_tensor(
                out=ds.rearrange("p (c i) t -> p c t i", i=LINE),
                in0=dpd[g][:, :, slots].rearrange("p t (c i) -> p c t i", i=LINE),
                in1=weights.rearrange("p t (c i) -> p c t i", i=LINE),
                op=ALU.mult,
            )

        def quantize_ds(g, slots, ds):
            quantize(ds_mx[g][0][:, slots], ds_mx[g][1][:, slots], ds.rearrange("p n t -> p (n t)"))

        def product(h, slots, bank, dk):
            acc = dk_psum.tile([P, HALF], F32, name="dk_acc", tag=bank)
            for g in range(PASSES):
                cols = slice(g * P, (g + 1) * P)
                nc.tensor.matmul_mx(
                    out=acc[:],
                    lhsT=q_mx[h][0][:, cols].bitcast(FP8X4),
                    lhsT_scale=q_mx[h][1][:, cols],
                    rhs=ds_mx[g][0][:, slots].bitcast(FP8X4),
                    rhs_scale=ds_mx[g][1][:, slots],
                    start=(g == 0),
                    stop=(g == PASSES - 1),
                )
            nc.scalar.copy(out=dk, in_=acc[:])

        def scatter(h, slots, dk):
            nc.vector.tensor_copy(window[h][:].indirect(offsets[:, slots.start // 16 : slots.stop // 16]), dk[:])

        ds = [keep.tile([P, N, PACK], BF16, name="ds%d" % g, align_bytes=64) for g in range(PASSES)]
        group_q(0)
        form_ds(0, first, p0a[:], ds[0][:, first, :])
        form_ds(0, second, p0b[:], ds[0][:, second, :])
        quantize_ds(0, first, ds[0][:, first, :])
        form_ds(1, first, p1a[:], ds[1][:, first, :])
        quantize_q(0)
        quantize_ds(1, first, ds[1][:, first, :])
        form_ds(1, second, p1b[:], ds[1][:, second, :])
        dk0a = keep.tile([P, HALF], F32, name="dk0a", tag="dk0a")
        product(0, first, "bank0", dk0a[:])
        quantize_ds(0, second, ds[0][:, second, :])
        quantize_ds(1, second, ds[1][:, second, :])
        dk0b = keep.tile([P, HALF], F32, name="dk0b")
        product(0, second, "bank1", dk0b[:])
        group_q(1)
        quantize_q(1)
        scatter(0, first, dk0a)
        dk1 = keep.tile([P, N], F32, name="dk1")
        product(1, first, "bank0", dk1[:, first])
        product(1, second, "bank2", dk1[:, second])
        scatter(0, second, dk0b)
        nc.sync.dma_start(out=out[0:P, :], in_=window[0][:])
        scatter(1, whole, dk1)
        nc.sync.dma_start(out=out[P : 2 * P, :], in_=window[1][:])
